import numpy as np
import ml_dtypes


def mxq(x, axis, fmt="e4m3"):
    dtype, down = {"e4m3": (ml_dtypes.float8_e4m3fn, 7), "e5m2": (ml_dtypes.float8_e5m2, 14)}[fmt]
    v = np.moveaxis(np.asarray(x, np.float32).astype(ml_dtypes.bfloat16).astype(np.float64), axis, -1)
    blocks = v.reshape(v.shape[:-1] + (-1, 32))
    amax = np.abs(blocks).max(-1, keepdims=True)
    byte = np.maximum(np.where(amax > 0, np.frexp(amax)[1] - 1 + 127, 0) - down, 1)
    scale = np.exp2(byte - 127.0)
    codes = (blocks / scale).astype(np.float32).astype(dtype).astype(np.float64)
    return np.moveaxis((codes * scale).reshape(v.shape), -1, axis)


WIDE = False


def mx_kscale(k):
    if not WIDE:
        return np.ones(k)
    levels = np.array([10, -10, 5, -5, 0])
    if k % 512:
        return np.exp2(np.random.permutation(np.resize(levels, k // 32))).repeat(32)
    a = np.empty((k // 512, 16))
    for p in range(k // 512):
        a[p, :8] = np.random.permutation(np.resize(levels, 8))
        for g in range(8):
            far = levels[np.abs(levels - a[p, g]) >= 10]
            a[p, g + 8] = far[np.random.randint(len(far))]
    return np.exp2(a.ravel()).repeat(32)


def f64(x):
    return np.asarray(x).astype(np.float64)


def striped(idx):
    return np.tile(idx.reshape(-1, 16).T, (8, 1)).astype(np.uint16)


def unstriped(offs):
    return offs[:16].T.reshape(-1).astype(np.int64)


def sigmoid(v):
    return 1.0 / (1.0 + np.exp(-np.maximum(v, -700.0)))


K, T, E, C, H, N = 512, 1024, 6, 128, 1024, 256


def by_expert(wq, xq):
    return np.concatenate([wq[e].T @ xq[:, e * C:(e + 1) * C] for e in range(E)], axis=1)


def setup_inputs():
    n = np.random.standard_normal
    s = mx_kscale(K)[:, None]
    u = mx_kscale(H)
    return {
        "xT": (n((K, T)) * s).astype(np.float32),
        "w1": (n((E, K, H)) / np.sqrt(K) / s[None]).astype(np.float32),
        "w3": (n((E, K, H)) / np.sqrt(K) / s[None] * u[None, None, :]).astype(np.float32),
        "w2": (n((E, H, N)) / np.sqrt(H) / u[None, :, None]).astype(np.float32),
        "gate": np.tile(np.random.uniform(0.2, 1.0, E * C), (N, 1)).astype(np.float32),
        "offs": striped(np.random.permutation(T)[:E * C]),
    }


def reference(xT, w1, w3, w2, gate, offs):
    idx = unstriped(offs)
    xq = mxq(f64(xT)[:, idx], 0, "e4m3")
    h = sigmoid(by_expert(mxq(f64(w1), 1, "e4m3"), xq))
    h = h * by_expert(mxq(f64(w3), 1, "e4m3"), xq)
    y = by_expert(mxq(f64(w2), 1, "e4m3"), mxq(h, 0, "e4m3"))
    out = np.zeros((N, T))
    out[:, idx] = f64(gate) * y
    return out

@@ -1,0 +1,260 @@
+from contextlib import ExitStack
+
+import concourse.mybir as mybir
+
+K, T, E, C, H, N = 512, 1024, 6, 128, 1024, 256
+S = E * C
+P = 128
+HALF = 512
+FLOPS = 2 * S * K * H * 2 + 2 * S * H * N
+
+F32 = mybir.dt.float32
+BF16 = mybir.dt.bfloat16
+U32 = mybir.dt.uint32
+U16 = mybir.dt.uint16
+U8 = mybir.dt.uint8
+FP8X4 = mybir.dt.float8_e4m3fn_x4
+MULT = mybir.AluOpType.mult
+SIGMOID = mybir.ActivationFunctionType.Sigmoid
+
+ORDER = """
+ldx:0 memwin ldof ldx:1 ld:w1:0:* cx:0:V qx:0 cx:1:V
+qx:1 ld:w3:0:* g1 g2 c:w1:0:1:S ld:w1:1:* c:w1:0:0:S c:w3:0:1:V
+q:w1:0:* ld:w3:1:* c:w3:0:0:V mm:a:0:0 mm:a:0:1 sig:0:0 q:w3:0:* sig:0:1
+c:w1:1:1:S mm:b:0:0 mm:b:0:1 mul:0:0 ldgate mul:0:1 qh:0:* c:w1:1:0:S
+ld:w2:0:* c:w3:1:0:V c:w3:1:1:V ld:w1:2:* q:w1:1:* q:w3:1:* c:w2:0:1:S mm:a:1:0
+mm:a:1:1 mm:b:1:0 c:w2:0:0:S mm:b:1:1 ld:w3:2:* sig:1:0 q:w2:0:* sig:1:1
+mul:1:0 mmy:0 c:w1:2:0:S mul:1:1 qh:1:* ld:w2:1:* c:w1:2:1:S ld:w1:3:*
+c:w3:2:1:V cy:0 c:w3:2:0:V c:w2:1:1:S q:w1:2:* c:w2:1:0:S q:w3:2:* mm:a:2:1
+ld:w3:3:* mm:a:2:0 sc:0:0 sig:2:1 mm:b:2:0 mm:b:2:1 sig:2:0 q:w2:1:*
+mul:2:1 c:w1:3:0:S mmy:1 mul:2:0 sc:0:1 ld:w2:2:* qh:2:* c:w1:3:1:S
+ld:w1:4:* c:w3:3:1:V cy:1 c:w3:3:0:V c:w2:2:1:S q:w1:3:* c:w2:2:0:S sc:1:0
+mm:a:3:1 ld:w3:4:* mm:a:3:0 q:w3:3:* sig:3:1 sig:3:0 q:w2:2:* mm:b:3:1
+mm:b:3:0 sc:1:1 c:w1:4:1:S mmy:2 mul:3:1 mul:3:0 ld:w2:3:* qh:3:*
+cy:2 c:w1:4:0:S sc:2:0 ld:w1:5:0 sc:2:1 c:w3:4:1:V q:w1:4:* ld:w1:5:1
+c:w2:3:1:S c:w3:4:0:V mm:a:4:0 c:w2:3:0:S mm:a:4:1 ld:w3:5:0 c:w1:5:0:V sig:4:1
+q:w3:4:* sig:4:0 ld:w3:5:1 c:w1:5:1:S q:w2:3:* mm:b:4:0 mm:b:4:1 q:w1:5:0
+mmy:3 mul:4:1 mm:a:5:0 ld:w2:4:* mul:4:0 cy:3 q:w1:5:1 sig:5:0
+c:w3:5:0:V mm:a:5:1 ld:w2:5:0 sig:5:1 c:w3:5:1:V ld:w2:5:1 q:w3:5:0 c:w2:4:1:S
+sc:3:1 mm:b:5:0 qh:4:* q:w3:5:1 c:w2:4:0:S mul:5:0 mm:b:5:1 c:w2:5:1:V:0
+c:w2:5:1:S:1 mul:5:1 q:w2:4:* c:w2:5:0:S qh:5:1 mmy:4 q:w2:5:1 qh:5:0
+cy:4 sc:3:0 q:w2:5:0 sc:4:0 mmy:5 cy:5 sc:4:1 sc:5:0
+sc:5:1 st:0 st:1
+"""
+
+
+def tile_routed_moe_kernel(tc, xT, w1, w3, w2, gate, offs, out):
+    nc = tc.nc
+    weights = {"w1": w1, "w3": w3, "w2": w2}
+
+    def cast(engine, dst, src):
+        if engine == "V":
+            nc.vector.tensor_copy(out=dst, in_=src)
+        else:
+            nc.scalar.copy(out=dst, in_=src)
+
+    def quantize(codes, scales, values):
+        nc.vector.quantize_mx(out=codes.bitcast(FP8X4), scales=scales, in_=values)
+
+    def plain(dst, src):
+        return dst.rearrange("p (c i j) -> p c j i", i=4, j=4), src.rearrange("p j (c i) -> p c j i", i=4)
+
+    def permuted(dst, src):
+        return dst.rearrange("p (t m j) -> p m j t", t=4, j=4), src.rearrange("p j (m t) -> p m j t", t=4)
+
+    with ExitStack() as ctx:
+        held = ctx.enter_context(tc.tile_pool(name="held", bufs=1))
+        rawp = ctx.enter_context(tc.tile_pool(name="raw", bufs=6))
+        raw2p = ctx.enter_context(tc.tile_pool(name="raw2", bufs=2))
+        grp = ctx.enter_context(tc.tile_pool(name="grp", bufs=2))
+        cod = ctx.enter_context(tc.tile_pool(name="cod", bufs=2))
+        act = ctx.enter_context(tc.tile_pool(name="act", bufs=2))
+        psab = ctx.enter_context(tc.psum_pool(name="psab", bufs=3))
+        psy = ctx.enter_context(tc.psum_pool(name="psy", bufs=2))
+
+        offs_t = held.tile([P, S // 16], U16, name="offs_t")
+        gate_t = held.tile([P, 2, S], F32, name="gate_t")
+        xq = held.tile([P, T], U32, name="xq", align_bytes=64)
+        xs = held.tile([P, T], U8, name="xs", align_bytes=64)
+        xgq = held.tile([P, S], U32, name="xgq", align_bytes=64)
+        xgs = held.tile([P, S], U8, name="xgs", align_bytes=64)
+        win = [held.tile([P, T], F32, name="win%d" % b) for b in range(2)]
+        live = {}
+
+        def get(key, make):
+            if key not in live:
+                live[key] = make()
+            return live[key]
+
+        def raw13(nm, e):
+            return get(("raw", nm, e), lambda: rawp.tile([P, 4, H], F32, name="raw"))
+
+        def raw2(e):
+            return get(("raw2", e), lambda: raw2p.tile([P, 2, 4, N], F32, name="raw2"))
+
+        def staged(nm, e):
+            if nm == "w2":
+                return get((nm + "g", e), lambda: grp.tile([P, 2, 4 * N], BF16, name="w2g", align_bytes=64))
+            return get((nm + "g", e), lambda: grp.tile([P, 4 * H], BF16, name=("w1g" if nm == "x" else nm + "g"), align_bytes=64))
+
+        def codes(nm, e):
+            shape = [P, 2, N] if nm == "w2" else [P, H]
+            c = get((nm + "c", e), lambda: cod.tile(shape, U32, name=nm + "c", align_bytes=64))
+            s = get((nm + "s", e), lambda: cod.tile(shape, U8, name=nm + "s", align_bytes=64))
+            return c, s
+
+        def hidden(e):
+            hq = get(("hq", e), lambda: act.tile([P, 2, C], U32, name="hq", align_bytes=64))
+            hs = get(("hs", e), lambda: act.tile([P, 2, C], U8, name="hs", align_bytes=64))
+            hb = get(("hb", e), lambda: act.tile([P, 2, C, 4], BF16, name="hb", align_bytes=64))
+            return hq, hs, hb
+
+        def sig(e, g):
+            return get(("sig", e, g), lambda: act.tile([P, C, 4], F32, name="sig%d" % g))
+
+        def bank(nm, e, g):
+            return get((nm, e, g), lambda: psab.tile([P, 4, C], F32, name=nm))
+
+        def ybank(e):
+            return get(("y", e), lambda: psy.tile([P, 2, C], F32, name="y"))
+
+        def ysb(e):
+            return get(("ysb", e), lambda: act.tile([P, 2, C], F32, name="ysb"))
+
+        def half(g):
+            return slice(g * HALF, (g + 1) * HALF)
+
+        def half4(g):
+            return slice(4 * g * HALF, 4 * (g + 1) * HALF)
+
+        def run(name):
+            part = name.split(":")
+            op, a = part[0], part[1:]
+            if op == "memwin":
+                nc.gpsimd.memset(xs[:], 0)
+                for b in range(2):
+                    nc.vector.memset(win[b][:], 0.0)
+            elif op == "ldof":
+                nc.sync.dma_start(out=offs_t[:], in_=offs)
+            elif op == "ldgate":
+                nc.sync.dma_start(out=gate_t[:], in_=gate.rearrange("(b p) j -> p b j", p=P))
+            elif op == "ldx":
+                g = int(a[0])
+                nc.sync.dma_start(out=raw13("x", 0)[:, :, half(g)], in_=xT.rearrange("(p j) n -> p j n", j=4)[:, :, half(g)])
+            elif op == "ld" and a[0] == "w2":
+                e = int(a[1])
+                r = w2[e].rearrange("(g p j) c -> p g j c", p=P, j=4)
+                if a[2] == "*":
+                    nc.sync.dma_start(out=raw2(e)[:], in_=r)
+                else:
+                    g = int(a[2])
+                    nc.sync.dma_start(out=raw2(e)[:, g, :, :], in_=r[:, g, :, :])
+            elif op == "ld":
+                e = int(a[1])
+                r = weights[a[0]][e].rearrange("(p j) c -> p j c", j=4)
+                if a[2] == "*":
+                    nc.sync.dma_start(out=raw13(a[0], e)[:], in_=r)
+                else:
+                    cols = half(int(a[2]))
+                    nc.sync.dma_start(out=raw13(a[0], e)[:, :, cols], in_=r[:, :, cols])
+            elif op == "cx":
+                g = int(a[0])
+                cast(a[1], *plain(staged("x", 0)[:, half4(g)], raw13("x", 0)[:, :, half(g)]))
+            elif op == "qx":
+                g = int(a[0])
+                quantize(xq[:, half(g)], xs[:, half(g)], staged("x", 0)[:, half4(g)])
+            elif op == "g1":
+                nc.vector.tensor_copy(out=xgq[:], in_=xq[:].indirect(offs_t[:]))
+            elif op == "g2":
+                nc.vector.tensor_copy(out=xgs[:], in_=xs[:].indirect(offs_t[:]))
+            elif op == "c" and a[0] == "w2":
+                e, g = int(a[1]), int(a[2])
+                if len(a) > 4:
+                    b = int(a[4])
+                    m = slice(b * P, (b + 1) * P)
+                    cast(a[3], *plain(staged("w2", e)[:, g, 4 * b * P : 4 * (b + 1) * P], raw2(e)[:, g, :, m]))
+                else:
+                    cast(a[3], *plain(staged("w2", e)[:, g, :], raw2(e)[:, g, :, :]))
+            elif op == "c":
+                e, g = int(a[1]), int(a[2])
+                cast(a[3], *permuted(staged(a[0], e)[:, half4(g)], raw13(a[0], e)[:, :, half(g)]))
+            elif op == "q" and a[0] == "w2":
+                e = int(a[1])
+                c, s = codes("w2", e)
+                w = staged("w2", e)
+                if a[2] == "*":
+                    quantize(c[:].rearrange("p g n -> p (g n)"), s[:].rearrange("p g n -> p (g n)"), w[:].rearrange("p g n -> p (g n)"))
+                else:
+                    g = int(a[2])
+                    quantize(c[:, g, :], s[:, g, :], w[:, g, :])
+            elif op == "q":
+                e = int(a[1])
+                c, s = codes(a[0], e)
+                w = staged(a[0], e)
+                if a[2] == "*":
+                    quantize(c[:], s[:], w[:])
+                else:
+                    g = int(a[2])
+                    quantize(c[:, half(g)], s[:, half(g)], w[:, half4(g)])
+            elif op == "mm":
+                e, g = int(a[1]), int(a[2])
+                c, s = codes({"a": "w1", "b": "w3"}[a[0]], e)
+                k = bank(a[0], e, g)
+                for t in range(4):
+                    m = slice(g * HALF + t * P, g * HALF + (t + 1) * P)
+                    nc.tensor.matmul_mx(
+                        out=k[:, t, :],
+                        lhsT=c[:, m].bitcast(FP8X4),
+                        lhsT_scale=s[:, m],
+                        rhs=xgq[:, e * C : (e + 1) * C].bitcast(FP8X4),
+                        rhs_scale=xgs[:, e * C : (e + 1) * C],
+                        start=True,
+                        stop=True,
+                    )
+            elif op == "sig":
+                e, g = int(a[0]), int(a[1])
+                nc.scalar.activation(out=sig(e, g)[:], in_=bank("a", e, g)[:].rearrange("p t n -> p n t"), func=SIGMOID)
+            elif op == "mul":
+                e, g = int(a[0]), int(a[1])
+                nc.vector.tensor_tensor(out=hidden(e)[2][:, g, :, :], in0=bank("b", e, g)[:].rearrange("p t n -> p n t"), in1=sig(e, g)[:], op=MULT)
+            elif op == "qh":
+                e = int(a[0])
+                hq, hs, hb = hidden(e)
+                if a[1] == "*":
+                    quantize(hq[:].rearrange("p g n -> p (g n)"), hs[:].rearrange("p g n -> p (g n)"), hb[:].rearrange("p g n t -> p (g n t)"))
+                else:
+                    g = int(a[1])
+                    quantize(hq[:, g, :], hs[:, g, :], hb[:, g, :, :].rearrange("p n t -> p (n t)"))
+            elif op == "mmy":
+                e = int(a[0])
+                hq, hs, hb = hidden(e)
+                c, s = codes("w2", e)
+                for b in range(2):
+                    for g in range(2):
+                        m = slice(b * P, (b + 1) * P)
+                        nc.tensor.matmul_mx(
+                            out=ybank(e)[:, b, :],
+                            lhsT=c[:, g, m].bitcast(FP8X4),
+                            lhsT_scale=s[:, g, m],
+                            rhs=hq[:, g, :].bitcast(FP8X4),
+                            rhs_scale=hs[:, g, :],
+                            start=(g == 0),
+                            stop=(g == 1),
+                        )
+            elif op == "cy":
+                e = int(a[0])
+                nc.scalar.copy(out=ysb(e)[:], in_=ybank(e)[:])
+            elif op == "sc":
+                e, b = int(a[0]), int(a[1])
+                nc.vector.tensor_tensor(
+                    out=win[b][:].indirect(offs_t[:, e * (C // 16) : (e + 1) * (C // 16)]),
+                    in0=ysb(e)[:, b, :],
+                    in1=gate_t[:, b, e * C : (e + 1) * C],
+                    op=MULT,
+                )
+            elif op == "st":
+                b = int(a[0])
+                nc.sync.dma_start(out=out[b * P : (b + 1) * P, :], in_=win[b][:])
+
+        for name in ORDER.split():
+            run(name)

@@ -18,27 +18,27 @@ MULT = mybir.AluOpType.mult
 SIGMOID = mybir.ActivationFunctionType.Sigmoid
 
 ORDER = """
-ldx:0 memwin ldof ldx:1 ld:w1:0:* cx:0:V qx:0 cx:1:V
-qx:1 ld:w3:0:* g1 g2 c:w1:0:1:S ld:w1:1:* c:w1:0:0:S c:w3:0:1:V
-q:w1:0:* ld:w3:1:* c:w3:0:0:V mm:a:0:0 mm:a:0:1 sig:0:0 q:w3:0:* sig:0:1
-c:w1:1:1:S mm:b:0:0 mm:b:0:1 mul:0:0 ldgate mul:0:1 qh:0:* c:w1:1:0:S
-ld:w2:0:* c:w3:1:0:V c:w3:1:1:V ld:w1:2:* q:w1:1:* q:w3:1:* c:w2:0:1:S mm:a:1:0
-mm:a:1:1 mm:b:1:0 c:w2:0:0:S mm:b:1:1 ld:w3:2:* sig:1:0 q:w2:0:* sig:1:1
-mul:1:0 mmy:0 c:w1:2:0:S mul:1:1 qh:1:* ld:w2:1:* c:w1:2:1:S ld:w1:3:*
-c:w3:2:1:V cy:0 c:w3:2:0:V c:w2:1:1:S q:w1:2:* c:w2:1:0:S q:w3:2:* mm:a:2:1
-ld:w3:3:* mm:a:2:0 sc:0:0 sig:2:1 mm:b:2:0 mm:b:2:1 sig:2:0 q:w2:1:*
-mul:2:1 c:w1:3:0:S mmy:1 mul:2:0 sc:0:1 ld:w2:2:* qh:2:* c:w1:3:1:S
-ld:w1:4:* c:w3:3:1:V cy:1 c:w3:3:0:V c:w2:2:1:S q:w1:3:* c:w2:2:0:S sc:1:0
-mm:a:3:1 ld:w3:4:* mm:a:3:0 q:w3:3:* sig:3:1 sig:3:0 q:w2:2:* mm:b:3:1
-mm:b:3:0 sc:1:1 c:w1:4:1:S mmy:2 mul:3:1 mul:3:0 ld:w2:3:* qh:3:*
-cy:2 c:w1:4:0:S sc:2:0 ld:w1:5:0 sc:2:1 c:w3:4:1:V q:w1:4:* ld:w1:5:1
-c:w2:3:1:S c:w3:4:0:V mm:a:4:0 c:w2:3:0:S mm:a:4:1 ld:w3:5:0 c:w1:5:0:V sig:4:1
-q:w3:4:* sig:4:0 ld:w3:5:1 c:w1:5:1:S q:w2:3:* mm:b:4:0 mm:b:4:1 q:w1:5:0
-mmy:3 mul:4:1 mm:a:5:0 ld:w2:4:* mul:4:0 cy:3 q:w1:5:1 sig:5:0
-c:w3:5:0:V mm:a:5:1 ld:w2:5:0 sig:5:1 c:w3:5:1:V ld:w2:5:1 q:w3:5:0 c:w2:4:1:S
-sc:3:1 mm:b:5:0 qh:4:* q:w3:5:1 c:w2:4:0:S mul:5:0 mm:b:5:1 c:w2:5:1:V:0
-c:w2:5:1:S:1 mul:5:1 q:w2:4:* c:w2:5:0:S qh:5:1 mmy:4 q:w2:5:1 qh:5:0
-cy:4 sc:3:0 q:w2:5:0 sc:4:0 mmy:5 cy:5 sc:4:1 sc:5:0
+ldx:0 memwin ldof ldx:1 cx:0:V qx:0 ld:w1:0:* cx:1:V
+qx:1 g1 ld:w3:0:* c:w1:0:0:S g2 c:w1:0:1:S ld:w1:1:* c:w3:0:1:V
+c:w3:0:0:V q:w1:0:* q:w3:0:* ld:w3:1:* mm:a:0:1 c:w1:1:0:S mm:a:0:0 c:w1:1:1:S
+mm:b:0:0 mm:b:0:1 ldgate c:w3:1:1:V sig:0:0 sig:0:1 ld:w2:0:* q:w1:1:*
+c:w3:1:0:V mm:a:1:0 ld:w1:2:* c:w2:0:0:S mul:0:1 mm:a:1:1 q:w3:1:* c:w2:0:1:S
+mul:0:0 sig:1:1 mm:b:1:0 sig:1:0 q:w2:0:* mm:b:1:1 qh:0:* ld:w3:2:*
+c:w1:2:0:S mul:1:0 mmy:0 mul:1:1 qh:1:* c:w1:2:1:S ld:w2:1:* c:w3:2:0:V
+cy:0 q:w1:2:* ld:w1:3:* c:w2:1:1:S c:w3:2:1:V mm:a:2:1 c:w2:1:0:S sc:0:0
+mm:a:2:0 sig:2:1 q:w3:2:* sig:2:0 ld:w3:3:* sc:0:1 c:w1:3:0:S mm:b:2:1
+q:w2:1:* mm:b:2:0 mul:2:1 c:w1:3:1:S mmy:1 mul:2:0 qh:2:* ld:w2:2:*
+c:w3:3:0:V cy:1 c:w3:3:1:V ld:w1:4:* c:w2:2:1:S q:w1:3:* c:w2:2:0:S q:w3:3:*
+mm:a:3:0 sc:1:1 mm:a:3:1 sig:3:0 ld:w3:4:* q:w2:2:* c:w1:4:1:S mm:b:3:1
+c:w1:4:0:V mmy:2 sc:1:0 sig:3:1 mm:b:3:0 cy:2 q:w1:4:* ld:w2:3:*
+c:w3:4:1:S c:w3:4:0:V mm:a:4:1 mul:3:1 mm:a:4:0 ld:w1:5:0 mul:3:0 c:w2:3:0:S
+q:w3:4:* sig:4:0 ld:w1:5:1 sig:4:1 c:w1:5:0:V mm:b:4:1 c:w2:3:1:S qh:3:*
+mm:b:4:0 ld:w3:5:0 mul:4:1 c:w1:5:1:S q:w1:5:0 mul:4:0 mm:a:5:0 ld:w3:5:1
+sc:2:1 sig:5:0 c:w3:5:0:V ld:w2:4:* c:w3:5:1:S q:w1:5:1 q:w3:5:0 mm:a:5:1
+qh:4:* ld:w2:5:0 q:w2:3:* c:w2:4:0:S mm:b:5:0 ld:w2:5:1 q:w3:5:1 sig:5:1
+mmy:3 sc:2:0 c:w2:5:0:S mul:5:0 mm:b:5:1 c:w2:5:1:S:1 q:w2:5:0 cy:3
+qh:5:0 c:w2:4:1:S c:w2:5:1:V:0 mul:5:1 q:w2:5:1 q:w2:4:* sc:3:0 mmy:4
+sc:3:1 cy:4 qh:5:1 sc:4:0 mmy:5 sc:4:1 cy:5 sc:5:0
 sc:5:1 st:0 st:1
 """
 

@@ -17,57 +17,30 @@ FP8X4 = mybir.dt.float8_e4m3fn_x4
 MULT = mybir.AluOpType.mult
 SIGMOID = mybir.ActivationFunctionType.Sigmoid
 
-ORDER = """
-ldx:0 memwin ldof ldx:1 cx:0:V qx:0 ld:w1:0:* cx:1:V
-qx:1 g1 ld:w3:0:* c:w1:0:0:S g2 c:w1:0:1:S ld:w1:1:* c:w3:0:1:V
-c:w3:0:0:V q:w1:0:* q:w3:0:* ld:w3:1:* mm:a:0:1 c:w1:1:0:S mm:a:0:0 c:w1:1:1:S
-mm:b:0:0 mm:b:0:1 ldgate c:w3:1:1:V sig:0:0 sig:0:1 ld:w2:0:* q:w1:1:*
-c:w3:1:0:V mm:a:1:0 ld:w1:2:* c:w2:0:0:S mul:0:1 mm:a:1:1 q:w3:1:* c:w2:0:1:S
-mul:0:0 sig:1:1 mm:b:1:0 sig:1:0 q:w2:0:* mm:b:1:1 qh:0:* ld:w3:2:*
-c:w1:2:0:S mul:1:0 mmy:0 mul:1:1 qh:1:* c:w1:2:1:S ld:w2:1:* c:w3:2:0:V
-cy:0 q:w1:2:* ld:w1:3:* c:w2:1:1:S c:w3:2:1:V mm:a:2:1 c:w2:1:0:S sc:0:0
-mm:a:2:0 sig:2:1 q:w3:2:* sig:2:0 ld:w3:3:* sc:0:1 c:w1:3:0:S mm:b:2:1
-q:w2:1:* mm:b:2:0 mul:2:1 c:w1:3:1:S mmy:1 mul:2:0 qh:2:* ld:w2:2:*
-c:w3:3:0:V cy:1 c:w3:3:1:V ld:w1:4:* c:w2:2:1:S q:w1:3:* c:w2:2:0:S q:w3:3:*
-mm:a:3:0 sc:1:1 mm:a:3:1 sig:3:0 ld:w3:4:* q:w2:2:* c:w1:4:1:S mm:b:3:1
-c:w1:4:0:V mmy:2 sc:1:0 sig:3:1 mm:b:3:0 cy:2 q:w1:4:* ld:w2:3:*
-c:w3:4:1:S c:w3:4:0:V mm:a:4:1 mul:3:1 mm:a:4:0 ld:w1:5:0 mul:3:0 c:w2:3:0:S
-q:w3:4:* sig:4:0 ld:w1:5:1 sig:4:1 c:w1:5:0:V mm:b:4:1 c:w2:3:1:S qh:3:*
-mm:b:4:0 ld:w3:5:0 mul:4:1 c:w1:5:1:S q:w1:5:0 mul:4:0 mm:a:5:0 ld:w3:5:1
-sc:2:1 sig:5:0 c:w3:5:0:V ld:w2:4:* c:w3:5:1:S q:w1:5:1 q:w3:5:0 mm:a:5:1
-qh:4:* ld:w2:5:0 q:w2:3:* c:w2:4:0:S mm:b:5:0 ld:w2:5:1 q:w3:5:1 sig:5:1
-mmy:3 sc:2:0 c:w2:5:0:S mul:5:0 mm:b:5:1 c:w2:5:1:S:1 q:w2:5:0 cy:3
-qh:5:0 c:w2:4:1:S c:w2:5:1:V:0 mul:5:1 q:w2:5:1 q:w2:4:* sc:3:0 mmy:4
-sc:3:1 cy:4 qh:5:1 sc:4:0 mmy:5 sc:4:1 cy:5 sc:5:0
-sc:5:1 st:0 st:1
-"""
-
 
 def tile_routed_moe_kernel(tc, xT, w1, w3, w2, gate, offs, out):
     nc = tc.nc
-    weights = {"w1": w1, "w3": w3, "w2": w2}
-
-    def cast(engine, dst, src):
-        if engine == "V":
-            nc.vector.tensor_copy(out=dst, in_=src)
-        else:
-            nc.scalar.copy(out=dst, in_=src)
 
     def quantize(codes, scales, values):
         nc.vector.quantize_mx(out=codes.bitcast(FP8X4), scales=scales, in_=values)
 
     def plain(dst, src):
-        return dst.rearrange("p (c i j) -> p c j i", i=4, j=4), src.rearrange("p j (c i) -> p c j i", i=4)
+        return dict(out=dst.rearrange("p (c i j) -> p c j i", i=4, j=4), in_=src.rearrange("p j (c i) -> p c j i", i=4))
 
     def permuted(dst, src):
-        return dst.rearrange("p (t m j) -> p m j t", t=4, j=4), src.rearrange("p j (m t) -> p m j t", t=4)
+        return dict(out=dst.rearrange("p (t m j) -> p m j t", t=4, j=4), in_=src.rearrange("p j (m t) -> p m j t", t=4))
+
+    def half(g):
+        return slice(g * HALF, (g + 1) * HALF)
+
+    def block(b):
+        return slice(b * P, (b + 1) * P)
 
     with ExitStack() as ctx:
         held = ctx.enter_context(tc.tile_pool(name="held", bufs=1))
-        rawp = ctx.enter_context(tc.tile_pool(name="raw", bufs=6))
-        raw2p = ctx.enter_context(tc.tile_pool(name="raw2", bufs=2))
-        grp = ctx.enter_context(tc.tile_pool(name="grp", bufs=2))
-        cod = ctx.enter_context(tc.tile_pool(name="cod", bufs=2))
+        rawp = ctx.enter_context(tc.tile_pool(name="rawp", bufs=7))
+        grp = ctx.enter_context(tc.tile_pool(name="grp", bufs=3))
+        cod = ctx.enter_context(tc.tile_pool(name="cod", bufs=3))
         act = ctx.enter_context(tc.tile_pool(name="act", bufs=2))
         psab = ctx.enter_context(tc.psum_pool(name="psab", bufs=3))
         psy = ctx.enter_context(tc.psum_pool(name="psy", bufs=2))
@@ -79,182 +52,166 @@ def tile_routed_moe_kernel(tc, xT, w1, w3, w2, gate, offs, out):
         xgq = held.tile([P, S], U32, name="xgq", align_bytes=64)
         xgs = held.tile([P, S], U8, name="xgs", align_bytes=64)
         win = [held.tile([P, T], F32, name="win%d" % b) for b in range(2)]
-        live = {}
+        warm = held.tile([P, 1], F32, name="warm")
+        warmed = held.tile([P, 1], F32, name="warmed")
 
-        def get(key, make):
-            if key not in live:
-                live[key] = make()
-            return live[key]
+        nc.gpsimd.memset(warm[:], 0.0)
+        nc.scalar.activation(out=warmed[:], in_=warm[:], func=SIGMOID)
+        nc.gpsimd.memset(xs[:], 0)
+        for b in range(2):
+            nc.vector.memset(win[b][:], 0.0)
 
-        def raw13(nm, e):
-            return get(("raw", nm, e), lambda: rawp.tile([P, 4, H], F32, name="raw"))
+        raws = {}
 
-        def raw2(e):
-            return get(("raw2", e), lambda: raw2p.tile([P, 2, 4, N], F32, name="raw2"))
+        def load(key, shape, src, queue=nc.sync):
+            raw = rawp.tile(shape, F32, name="raw")
+            queue.dma_start(out=raw[:], in_=src)
+            raws[key] = raw
 
-        def staged(nm, e):
-            if nm == "w2":
-                return get((nm + "g", e), lambda: grp.tile([P, 2, 4 * N], BF16, name="w2g", align_bytes=64))
-            return get((nm + "g", e), lambda: grp.tile([P, 4 * H], BF16, name=("w1g" if nm == "x" else nm + "g"), align_bytes=64))
+        def load13(e):
+            views = [w[e].rearrange("(p j) c -> p j c", j=4) for w in (w1, w3)]
+            if e in (5,):
+                for g in range(2):
+                    for i in range(2):
+                        load((i, e, g), [P, 4, HALF], views[i][:, :, half(g)], (nc.sync, nc.scalar)[i])
+            else:
+                for i in range(2):
+                    load((i, e), [P, 4, H], views[i], (nc.sync, nc.scalar)[i])
 
-        def codes(nm, e):
-            shape = [P, 2, N] if nm == "w2" else [P, H]
-            c = get((nm + "c", e), lambda: cod.tile(shape, U32, name=nm + "c", align_bytes=64))
-            s = get((nm + "s", e), lambda: cod.tile(shape, U8, name=nm + "s", align_bytes=64))
-            return c, s
+        def raw13(i, e, g):
+            if (i, e) in raws:
+                return raws[i, e][:, :, half(g)]
+            return raws[i, e, g][:]
 
-        def hidden(e):
-            hq = get(("hq", e), lambda: act.tile([P, 2, C], U32, name="hq", align_bytes=64))
-            hs = get(("hs", e), lambda: act.tile([P, 2, C], U8, name="hs", align_bytes=64))
-            hb = get(("hb", e), lambda: act.tile([P, 2, C, 4], BF16, name="hb", align_bytes=64))
-            return hq, hs, hb
+        def load2(e):
+            w2r = w2[e].rearrange("(g p j) c -> p g j c", p=P, j=4)
+            if e == E - 1:
+                for g in range(2):
+                    load((2, e, g), [P, 4, N], w2r[:, g, :, :])
+            else:
+                load((2, e), [P, 2, 4, N], w2r)
 
-        def sig(e, g):
-            return get(("sig", e, g), lambda: act.tile([P, C, 4], F32, name="sig%d" % g))
-
-        def bank(nm, e, g):
-            return get((nm, e, g), lambda: psab.tile([P, 4, C], F32, name=nm))
-
-        def ybank(e):
-            return get(("y", e), lambda: psy.tile([P, 2, C], F32, name="y"))
-
-        def ysb(e):
-            return get(("ysb", e), lambda: act.tile([P, 2, C], F32, name="ysb"))
-
-        def half(g):
-            return slice(g * HALF, (g + 1) * HALF)
-
-        def half4(g):
-            return slice(4 * g * HALF, 4 * (g + 1) * HALF)
-
-        def run(name):
-            part = name.split(":")
-            op, a = part[0], part[1:]
-            if op == "memwin":
-                nc.gpsimd.memset(xs[:], 0)
-                for b in range(2):
-                    nc.vector.memset(win[b][:], 0.0)
-            elif op == "ldof":
-                nc.sync.dma_start(out=offs_t[:], in_=offs)
-            elif op == "ldgate":
-                nc.sync.dma_start(out=gate_t[:], in_=gate.rearrange("(b p) j -> p b j", p=P))
-            elif op == "ldx":
-                g = int(a[0])
-                nc.sync.dma_start(out=raw13("x", 0)[:, :, half(g)], in_=xT.rearrange("(p j) n -> p j n", j=4)[:, :, half(g)])
-            elif op == "ld" and a[0] == "w2":
-                e = int(a[1])
-                r = w2[e].rearrange("(g p j) c -> p g j c", p=P, j=4)
-                if a[2] == "*":
-                    nc.sync.dma_start(out=raw2(e)[:], in_=r)
-                else:
-                    g = int(a[2])
-                    nc.sync.dma_start(out=raw2(e)[:, g, :, :], in_=r[:, g, :, :])
-            elif op == "ld":
-                e = int(a[1])
-                r = weights[a[0]][e].rearrange("(p j) c -> p j c", j=4)
-                if a[2] == "*":
-                    nc.sync.dma_start(out=raw13(a[0], e)[:], in_=r)
-                else:
-                    cols = half(int(a[2]))
-                    nc.sync.dma_start(out=raw13(a[0], e)[:, :, cols], in_=r[:, :, cols])
-            elif op == "cx":
-                g = int(a[0])
-                cast(a[1], *plain(staged("x", 0)[:, half4(g)], raw13("x", 0)[:, :, half(g)]))
-            elif op == "qx":
-                g = int(a[0])
-                quantize(xq[:, half(g)], xs[:, half(g)], staged("x", 0)[:, half4(g)])
-            elif op == "g1":
-                nc.vector.tensor_copy(out=xgq[:], in_=xq[:].indirect(offs_t[:]))
-            elif op == "g2":
-                nc.vector.tensor_copy(out=xgs[:], in_=xs[:].indirect(offs_t[:]))
-            elif op == "c" and a[0] == "w2":
-                e, g = int(a[1]), int(a[2])
-                if len(a) > 4:
-                    b = int(a[4])
-                    m = slice(b * P, (b + 1) * P)
-                    cast(a[3], *plain(staged("w2", e)[:, g, 4 * b * P : 4 * (b + 1) * P], raw2(e)[:, g, :, m]))
-                else:
-                    cast(a[3], *plain(staged("w2", e)[:, g, :], raw2(e)[:, g, :, :]))
-            elif op == "c":
-                e, g = int(a[1]), int(a[2])
-                cast(a[3], *permuted(staged(a[0], e)[:, half4(g)], raw13(a[0], e)[:, :, half(g)]))
-            elif op == "q" and a[0] == "w2":
-                e = int(a[1])
-                c, s = codes("w2", e)
-                w = staged("w2", e)
-                if a[2] == "*":
-                    quantize(c[:].rearrange("p g n -> p (g n)"), s[:].rearrange("p g n -> p (g n)"), w[:].rearrange("p g n -> p (g n)"))
-                else:
-                    g = int(a[2])
-                    quantize(c[:, g, :], s[:, g, :], w[:, g, :])
-            elif op == "q":
-                e = int(a[1])
-                c, s = codes(a[0], e)
-                w = staged(a[0], e)
-                if a[2] == "*":
-                    quantize(c[:], s[:], w[:])
-                else:
-                    g = int(a[2])
-                    quantize(c[:, half(g)], s[:, half(g)], w[:, half4(g)])
-            elif op == "mm":
-                e, g = int(a[1]), int(a[2])
-                c, s = codes({"a": "w1", "b": "w3"}[a[0]], e)
-                k = bank(a[0], e, g)
-                for t in range(4):
-                    m = slice(g * HALF + t * P, g * HALF + (t + 1) * P)
-                    nc.tensor.matmul_mx(
-                        out=k[:, t, :],
-                        lhsT=c[:, m].bitcast(FP8X4),
-                        lhsT_scale=s[:, m],
-                        rhs=xgq[:, e * C : (e + 1) * C].bitcast(FP8X4),
-                        rhs_scale=xgs[:, e * C : (e + 1) * C],
-                        start=True,
-                        stop=True,
-                    )
-            elif op == "sig":
-                e, g = int(a[0]), int(a[1])
-                nc.scalar.activation(out=sig(e, g)[:], in_=bank("a", e, g)[:].rearrange("p t n -> p n t"), func=SIGMOID)
-            elif op == "mul":
-                e, g = int(a[0]), int(a[1])
-                nc.vector.tensor_tensor(out=hidden(e)[2][:, g, :, :], in0=bank("b", e, g)[:].rearrange("p t n -> p n t"), in1=sig(e, g)[:], op=MULT)
-            elif op == "qh":
-                e = int(a[0])
-                hq, hs, hb = hidden(e)
-                if a[1] == "*":
-                    quantize(hq[:].rearrange("p g n -> p (g n)"), hs[:].rearrange("p g n -> p (g n)"), hb[:].rearrange("p g n t -> p (g n t)"))
-                else:
-                    g = int(a[1])
-                    quantize(hq[:, g, :], hs[:, g, :], hb[:, g, :, :].rearrange("p n t -> p (n t)"))
-            elif op == "mmy":
-                e = int(a[0])
-                hq, hs, hb = hidden(e)
-                c, s = codes("w2", e)
-                for b in range(2):
-                    for g in range(2):
-                        m = slice(b * P, (b + 1) * P)
+        def first(e):
+            staged = []
+            for g in range(2):
+                st = grp.tile([P, 2, 4 * HALF], BF16, name="st", align_bytes=64)
+                nc.scalar.copy(**permuted(st[:, 0, :], raw13(0, e, g)))
+                nc.vector.tensor_copy(**permuted(st[:, 1, :], raw13(1, e, g)))
+                staged.append(st)
+            banks, sigs = [], []
+            for g in range(2):
+                codes = cod.tile([P, 2, HALF], U32, name="codes", align_bytes=64)
+                scales = cod.tile([P, 2, HALF], U8, name="scales", align_bytes=64)
+                quantize(
+                    codes[:].rearrange("p w c -> p (w c)"),
+                    scales[:].rearrange("p w c -> p (w c)"),
+                    staged[g][:].rearrange("p w c -> p (w c)"),
+                )
+                pair = [psab.tile([P, 4, C], F32, name="ab"[i]) for i in range(2)]
+                for i in range(2):
+                    for t in range(4):
                         nc.tensor.matmul_mx(
-                            out=ybank(e)[:, b, :],
-                            lhsT=c[:, g, m].bitcast(FP8X4),
-                            lhsT_scale=s[:, g, m],
-                            rhs=hq[:, g, :].bitcast(FP8X4),
-                            rhs_scale=hs[:, g, :],
-                            start=(g == 0),
-                            stop=(g == 1),
+                            out=pair[i][:, t, :],
+                            lhsT=codes[:, i, block(t)].bitcast(FP8X4),
+                            lhsT_scale=scales[:, i, block(t)],
+                            rhs=xgq[:, block(e)].bitcast(FP8X4),
+                            rhs_scale=xgs[:, block(e)],
+                            start=True,
+                            stop=True,
                         )
-            elif op == "cy":
-                e = int(a[0])
-                nc.scalar.copy(out=ysb(e)[:], in_=ybank(e)[:])
-            elif op == "sc":
-                e, b = int(a[0]), int(a[1])
+                sig = act.tile([P, C, 4], F32, name="sig%d" % g)
+                nc.scalar.activation(out=sig[:], in_=pair[0][:].rearrange("p t n -> p n t"), func=SIGMOID)
+                banks.append(pair[1])
+                sigs.append(sig)
+            return banks, sigs
+
+        def product(e, banks, sigs):
+            hb = act.tile([P, 2, C, 4], BF16, name="hb", align_bytes=64)
+            hq = act.tile([P, 2, C], U32, name="hq", align_bytes=64)
+            hs = act.tile([P, 2, C], U8, name="hs", align_bytes=64)
+            for g in range(2):
+                nc.vector.tensor_tensor(out=hb[:, g, :, :], in0=banks[g][:].rearrange("p t n -> p n t"), in1=sigs[g][:], op=MULT)
+                if e == E - 1:
+                    quantize(hq[:, g, :], hs[:, g, :], hb[:, g, :, :].rearrange("p n t -> p (n t)"))
+            if e < E - 1:
+                quantize(
+                    hq[:].rearrange("p g n -> p (g n)"),
+                    hs[:].rearrange("p g n -> p (g n)"),
+                    hb[:].rearrange("p g n t -> p (g n t)"),
+                )
+            return hq, hs
+
+        def make2(e):
+            codes = act.tile([P, 2, N], U32, name="w2c", align_bytes=64)
+            scales = act.tile([P, 2, N], U8, name="w2s", align_bytes=64)
+            st = act.tile([P, 2, 4 * N], BF16, name="w2g", align_bytes=64)
+            for g in range(2):
+                src = raws[2, e][:, g, :, :] if (2, e) in raws else raws[2, e, g][:]
+                nc.scalar.copy(**plain(st[:, g, :], src))
+                if e == E - 1:
+                    quantize(codes[:, g, :], scales[:, g, :], st[:, g, :])
+            if e < E - 1:
+                quantize(
+                    codes[:].rearrange("p g n -> p (g n)"),
+                    scales[:].rearrange("p g n -> p (g n)"),
+                    st[:].rearrange("p g n -> p (g n)"),
+                )
+            return codes, scales
+
+        def second(e, hidden, weights):
+            hq, hs = hidden
+            codes, scales = weights
+            y = psy.tile([P, 2, C], F32, name="y")
+            for b in range(2):
+                for g in range(2):
+                    nc.tensor.matmul_mx(
+                        out=y[:, b, :],
+                        lhsT=codes[:, g, block(b)].bitcast(FP8X4),
+                        lhsT_scale=scales[:, g, block(b)],
+                        rhs=hq[:, g, :].bitcast(FP8X4),
+                        rhs_scale=hs[:, g, :],
+                        start=(g == 0),
+                        stop=(g == 1),
+                    )
+            ysb = act.tile([P, 2, C], F32, name="ysb")
+            nc.scalar.copy(out=ysb[:], in_=y[:])
+            for b in range(2):
                 nc.vector.tensor_tensor(
                     out=win[b][:].indirect(offs_t[:, e * (C // 16) : (e + 1) * (C // 16)]),
-                    in0=ysb(e)[:, b, :],
-                    in1=gate_t[:, b, e * C : (e + 1) * C],
+                    in0=ysb[:, b, :],
+                    in1=gate_t[:, b, block(e)],
                     op=MULT,
                 )
-            elif op == "st":
-                b = int(a[0])
-                nc.sync.dma_start(out=out[b * P : (b + 1) * P, :], in_=win[b][:])
 
-        for name in ORDER.split():
-            run(name)
+        xr = xT.rearrange("(p j) n -> p j n", j=4)
+        for h in range(2):
+            load(("x", h), [P, 4, HALF], xr[:, :, half(h)])
+            if h == 0:
+                nc.sync.dma_start(out=offs_t[:], in_=offs)
+        for h in range(2):
+            st = grp.tile([P, 4 * HALF], BF16, name="st", align_bytes=64)
+            nc.vector.tensor_copy(**plain(st[:], raws["x", h][:]))
+            quantize(xq[:, half(h)], xs[:, half(h)], st[:])
+        nc.vector.tensor_copy(out=xgq[:], in_=xq[:].indirect(offs_t[:]))
+        nc.vector.tensor_copy(out=xgs[:], in_=xs[:].indirect(offs_t[:]))
+
+        hidden = None
+        for e in range(E):
+            if e == E - 1:
+                load2(e - 1)
+            load13(e)
+            if e == 1:
+                nc.sync.dma_start(out=gate_t[:], in_=gate.rearrange("(b p) j -> p b j", p=P))
+            if 0 < e < E - 1:
+                load2(e - 1)
+            banks, sigs = first(e)
+            if e > 0:
+                weights = make2(e - 1)
+            now = product(e, banks, sigs)
+            if e > 0:
+                second(e - 1, hidden, weights)
+            hidden = now
+        load2(E - 1)
+        second(E - 1, hidden, make2(E - 1))
+        for b in range(2):
+            nc.sync.dma_start(out=out[block(b), :], in_=win[b][:])

@@ -70,13 +70,13 @@ def tile_routed_moe_kernel(tc, xT, w1, w3, w2, gate, offs, out):
 
         def load13(e):
             views = [w[e].rearrange("(p j) c -> p j c", j=4) for w in (w1, w3)]
-            if e in (5,):
+            if e in (0, 5):
                 for g in range(2):
                     for i in range(2):
-                        load((i, e, g), [P, 4, HALF], views[i][:, :, half(g)], (nc.sync, nc.scalar)[i])
+                        load((i, e, g), [P, 4, HALF], views[i][:, :, half(g)])
             else:
                 for i in range(2):
-                    load((i, e), [P, 4, H], views[i], (nc.sync, nc.scalar)[i])
+                    load((i, e), [P, 4, H], views[i])
 
         def raw13(i, e, g):
             if (i, e) in raws:

from contextlib import ExitStack

import concourse.mybir as mybir

K, T, E, C, H, N = 512, 1024, 6, 128, 1024, 256
S = E * C
P = 128
HALF = 512
FLOPS = 2 * S * K * H * 2 + 2 * S * H * N

F32 = mybir.dt.float32
BF16 = mybir.dt.bfloat16
U32 = mybir.dt.uint32
U16 = mybir.dt.uint16
U8 = mybir.dt.uint8
FP8X4 = mybir.dt.float8_e4m3fn_x4
MULT = mybir.AluOpType.mult
SIGMOID = mybir.ActivationFunctionType.Sigmoid


def tile_routed_moe_kernel(tc, xT, w1, w3, w2, gate, offs, out):
    nc = tc.nc

    def quantize(codes, scales, values):
        nc.vector.quantize_mx(out=codes.bitcast(FP8X4), scales=scales, in_=values)

    def plain(dst, src):
        return dict(out=dst.rearrange("p (c i j) -> p c j i", i=4, j=4), in_=src.rearrange("p j (c i) -> p c j i", i=4))

    def permuted(dst, src):
        return dict(out=dst.rearrange("p (t m j) -> p m j t", t=4, j=4), in_=src.rearrange("p j (m t) -> p m j t", t=4))

    def half(g):
        return slice(g * HALF, (g + 1) * HALF)

    def block(b):
        return slice(b * P, (b + 1) * P)

    with ExitStack() as ctx:
        held = ctx.enter_context(tc.tile_pool(name="held", bufs=1))
        rawp = ctx.enter_context(tc.tile_pool(name="rawp", bufs=7))
        grp = ctx.enter_context(tc.tile_pool(name="grp", bufs=3))
        cod = ctx.enter_context(tc.tile_pool(name="cod", bufs=3))
        act = ctx.enter_context(tc.tile_pool(name="act", bufs=2))
        psab = ctx.enter_context(tc.psum_pool(name="psab", bufs=3))
        psy = ctx.enter_context(tc.psum_pool(name="psy", bufs=2))

        offs_t = held.tile([P, S // 16], U16, name="offs_t")
        gate_t = held.tile([P, 2, S], F32, name="gate_t")
        xq = held.tile([P, T], U32, name="xq", align_bytes=64)
        xs = held.tile([P, T], U8, name="xs", align_bytes=64)
        xgq = held.tile([P, S], U32, name="xgq", align_bytes=64)
        xgs = held.tile([P, S], U8, name="xgs", align_bytes=64)
        win = [held.tile([P, T], F32, name="win%d" % b) for b in range(2)]
        warm = held.tile([P, 1], F32, name="warm")
        warmed = held.tile([P, 1], F32, name="warmed")

        nc.gpsimd.memset(warm[:], 0.0)
        nc.scalar.activation(out=warmed[:], in_=warm[:], func=SIGMOID)
        nc.gpsimd.memset(xs[:], 0)
        for b in range(2):
            nc.vector.memset(win[b][:], 0.0)

        raws = {}

        def load(key, shape, src, queue=nc.sync):
            raw = rawp.tile(shape, F32, name="raw")
            queue.dma_start(out=raw[:], in_=src)
            raws[key] = raw

        def load13(e):
            views = [w[e].rearrange("(p j) c -> p j c", j=4) for w in (w1, w3)]
            if e in (0, 5):
                for g in range(2):
                    for i in range(2):
                        load((i, e, g), [P, 4, HALF], views[i][:, :, half(g)])
            else:
                for i in range(2):
                    load((i, e), [P, 4, H], views[i])

        def raw13(i, e, g):
            if (i, e) in raws:
                return raws[i, e][:, :, half(g)]
            return raws[i, e, g][:]

        def load2(e):
            w2r = w2[e].rearrange("(g p j) c -> p g j c", p=P, j=4)
            if e == E - 1:
                for g in range(2):
                    load((2, e, g), [P, 4, N], w2r[:, g, :, :])
            else:
                load((2, e), [P, 2, 4, N], w2r)

        def first(e):
            staged = []
            for g in range(2):
                st = grp.tile([P, 2, 4 * HALF], BF16, name="st", align_bytes=64)
                nc.scalar.copy(**permuted(st[:, 0, :], raw13(0, e, g)))
                nc.vector.tensor_copy(**permuted(st[:, 1, :], raw13(1, e, g)))
                staged.append(st)
            banks, sigs = [], []
            for g in range(2):
                codes = cod.tile([P, 2, HALF], U32, name="codes", align_bytes=64)
                scales = cod.tile([P, 2, HALF], U8, name="scales", align_bytes=64)
                quantize(
                    codes[:].rearrange("p w c -> p (w c)"),
                    scales[:].rearrange("p w c -> p (w c)"),
                    staged[g][:].rearrange("p w c -> p (w c)"),
                )
                pair = [psab.tile([P, 4, C], F32, name="ab"[i]) for i in range(2)]
                for i in range(2):
                    for t in range(4):
                        nc.tensor.matmul_mx(
                            out=pair[i][:, t, :],
                            lhsT=codes[:, i, block(t)].bitcast(FP8X4),
                            lhsT_scale=scales[:, i, block(t)],
                            rhs=xgq[:, block(e)].bitcast(FP8X4),
                            rhs_scale=xgs[:, block(e)],
                            start=True,
                            stop=True,
                        )
                sig = act.tile([P, C, 4], F32, name="sig%d" % g)
                nc.scalar.activation(out=sig[:], in_=pair[0][:].rearrange("p t n -> p n t"), func=SIGMOID)
                banks.append(pair[1])
                sigs.append(sig)
            return banks, sigs

        def product(e, banks, sigs):
            hb = act.tile([P, 2, C, 4], BF16, name="hb", align_bytes=64)
            hq = act.tile([P, 2, C], U32, name="hq", align_bytes=64)
            hs = act.tile([P, 2, C], U8, name="hs", align_bytes=64)
            for g in range(2):
                nc.vector.tensor_tensor(out=hb[:, g, :, :], in0=banks[g][:].rearrange("p t n -> p n t"), in1=sigs[g][:], op=MULT)
                if e == E - 1:
                    quantize(hq[:, g, :], hs[:, g, :], hb[:, g, :, :].rearrange("p n t -> p (n t)"))
            if e < E - 1:
                quantize(
                    hq[:].rearrange("p g n -> p (g n)"),
                    hs[:].rearrange("p g n -> p (g n)"),
                    hb[:].rearrange("p g n t -> p (g n t)"),
                )
            return hq, hs

        def make2(e):
            codes = act.tile([P, 2, N], U32, name="w2c", align_bytes=64)
            scales = act.tile([P, 2, N], U8, name="w2s", align_bytes=64)
            st = act.tile([P, 2, 4 * N], BF16, name="w2g", align_bytes=64)
            for g in range(2):
                src = raws[2, e][:, g, :, :] if (2, e) in raws else raws[2, e, g][:]
                nc.scalar.copy(**plain(st[:, g, :], src))
                if e == E - 1:
                    quantize(codes[:, g, :], scales[:, g, :], st[:, g, :])
            if e < E - 1:
                quantize(
                    codes[:].rearrange("p g n -> p (g n)"),
                    scales[:].rearrange("p g n -> p (g n)"),
                    st[:].rearrange("p g n -> p (g n)"),
                )
            return codes, scales

        def second(e, hidden, weights):
            hq, hs = hidden
            codes, scales = weights
            y = psy.tile([P, 2, C], F32, name="y")
            for b in range(2):
                for g in range(2):
                    nc.tensor.matmul_mx(
                        out=y[:, b, :],
                        lhsT=codes[:, g, block(b)].bitcast(FP8X4),
                        lhsT_scale=scales[:, g, block(b)],
                        rhs=hq[:, g, :].bitcast(FP8X4),
                        rhs_scale=hs[:, g, :],
                        start=(g == 0),
                        stop=(g == 1),
                    )
            ysb = act.tile([P, 2, C], F32, name="ysb")
            nc.scalar.copy(out=ysb[:], in_=y[:])
            for b in range(2):
                nc.vector.tensor_tensor(
                    out=win[b][:].indirect(offs_t[:, e * (C // 16) : (e + 1) * (C // 16)]),
                    in0=ysb[:, b, :],
                    in1=gate_t[:, b, block(e)],
                    op=MULT,
                )

        xr = xT.rearrange("(p j) n -> p j n", j=4)
        for h in range(2):
            load(("x", h), [P, 4, HALF], xr[:, :, half(h)])
            if h == 0:
                nc.sync.dma_start(out=offs_t[:], in_=offs)
        for h in range(2):
            st = grp.tile([P, 4 * HALF], BF16, name="st", align_bytes=64)
            nc.vector.tensor_copy(**plain(st[:], raws["x", h][:]))
            quantize(xq[:, half(h)], xs[:, half(h)], st[:])
        nc.vector.tensor_copy(out=xgq[:], in_=xq[:].indirect(offs_t[:]))
        nc.vector.tensor_copy(out=xgs[:], in_=xs[:].indirect(offs_t[:]))

        hidden = None
        for e in range(E):
            if e == E - 1:
                load2(e - 1)
            load13(e)
            if e == 1:
                nc.sync.dma_start(out=gate_t[:], in_=gate.rearrange("(b p) j -> p b j", p=P))
            if 0 < e < E - 1:
                load2(e - 1)
            banks, sigs = first(e)
            if e > 0:
                weights = make2(e - 1)
            now = product(e, banks, sigs)
            if e > 0:
                second(e - 1, hidden, weights)
            hidden = now
        load2(E - 1)
        second(E - 1, hidden, make2(E - 1))
        for b in range(2):
            nc.sync.dma_start(out=out[block(b), :], in_=win[b][:])
